import numpy as np
import ml_dtypes


def mxq(x, axis, fmt="e4m3"):
    dtype, down = {"e4m3": (ml_dtypes.float8_e4m3fn, 7), "e5m2": (ml_dtypes.float8_e5m2, 14)}[fmt]
    v = np.moveaxis(np.asarray(x, np.float32).astype(ml_dtypes.bfloat16).astype(np.float64), axis, -1)
    blocks = v.reshape(v.shape[:-1] + (-1, 32))
    amax = np.abs(blocks).max(-1, keepdims=True)
    byte = np.maximum(np.where(amax > 0, np.frexp(amax)[1] - 1 + 127, 0) - down, 1)
    scale = np.exp2(byte - 127.0)
    codes = (blocks / scale).astype(np.float32).astype(dtype).astype(np.float64)
    return np.moveaxis((codes * scale).reshape(v.shape), -1, axis)


WIDE = False


def mx_kscale(k):
    if not WIDE:
        return np.ones(k)
    levels = np.array([10, -10, 5, -5, 0])
    if k % 512:
        return np.exp2(np.random.permutation(np.resize(levels, k // 32))).repeat(32)
    a = np.empty((k // 512, 16))
    for p in range(k // 512):
        a[p, :8] = np.random.permutation(np.resize(levels, 8))
        for g in range(8):
            far = levels[np.abs(levels - a[p, g]) >= 10]
            a[p, g + 8] = far[np.random.randint(len(far))]
    return np.exp2(a.ravel()).repeat(32)


def f64(x):
    return np.asarray(x).astype(np.float64)


def striped8(idx):
    return np.asarray(idx).reshape(8, -1, 16).transpose(0, 2, 1).reshape(128, -1).astype(np.uint16)


def unstriped8(offs):
    return offs.reshape(8, 16, -1).transpose(0, 2, 1).reshape(8, -1).astype(np.int64)


def pick8(x, idx, run):
    r = np.arange(len(x))
    return x[r[:, None], idx[r % (8 * run) // run]]


E2M1 = np.array([0.0, 0.5, 1.0, 1.5, 2.0, 3.0, 4.0, 6.0, -0.0, -0.5, -1.0, -1.5, -2.0, -3.0, -4.0, -6.0])


def pack_weight(w, fmt):
    k, n = w.shape
    w = f64(np.asarray(w, np.float32).astype(ml_dtypes.bfloat16)).reshape(k // 32, 32, n)
    amax = np.abs(w).max(1)
    if fmt == "e4m3":
        byte = np.frexp(amax)[1] - 1 + 127 - 7
    else:
        mant, ex = np.frexp(amax / 6.0)
        byte = np.where(mant > 0.5, ex, ex - 1) + 127
    byte = np.clip(np.where(amax > 0, byte, 1), 1, 254)
    scaled = (w * np.exp2(127.0 - byte)[:, None, :]).reshape(k, n).astype(np.float32)
    by_word = np.ascontiguousarray(scaled.reshape(k // 512, 128, 4, n).transpose(0, 1, 3, 2))
    if fmt == "e4m3":
        words = by_word.astype(ml_dtypes.float8_e4m3fn).view(np.uint8)
    else:
        c = by_word.astype(ml_dtypes.float4_e2m1fn).view(np.uint8) & 0xF
        words = (c[..., 0::2] | (c[..., 1::2] << 4)).reshape(k // 512, 128, 2 * n)
    return np.ascontiguousarray(words), np.ascontiguousarray(byte.astype(np.uint8).reshape(k // 512, 16, n))


def unpack_weight(words, scales, fmt):
    g, _, n = scales.shape
    words = np.ascontiguousarray(words).reshape(g, 128, n, -1)
    if fmt == "e4m3":
        vals = words.view(ml_dtypes.float8_e4m3fn).astype(np.float64)
    else:
        nib = np.empty((g, 128, n, 4), np.uint8)
        nib[..., 0::2] = words & 0xF
        nib[..., 1::2] = words >> 4
        vals = E2M1[nib]
    vals = vals * np.repeat(np.exp2(scales.astype(np.float64) - 127.0), 8, axis=1)[..., None]
    return vals.transpose(0, 1, 3, 2).reshape(g * 512, n)


D, T, I, Q = 512, 1024, 512, 128


def setup_inputs():
    n = np.random.standard_normal
    idx = np.stack([np.random.permutation(T)[:I] for _ in range(8)])
    idx2 = np.stack([np.random.permutation(T)[:I] for _ in range(8)])
    idx3 = np.stack([np.random.permutation(T)[:I] for _ in range(8)])
    fd = mx_kscale(D)
    keysp = pack_weight(n((D, T)) / fd[:, None], "e2m1")
    return {
        "query": (n((D, Q)) * 0.9 / np.sqrt(D) * fd[:, None]).astype(np.float32),
        "query2": (n((D, Q)) * 0.9 / np.sqrt(D) * fd[:, None]).astype(np.float32),
        "keys_words": keysp[0],
        "keys_scales": keysp[1],
        "lam": (np.random.uniform(0.5, 1.3, (Q, 1))).astype(np.float32),
        "width": (np.random.uniform(0.3, 0.8, (Q, 1))).astype(np.float32),
        "old": (1.0 * n((Q, T))).astype(np.float32),
        "offs": striped8(idx),
        "offs2": striped8(idx2),
        "offs3": striped8(idx3),
    }


def reference(query, query2, keys_words, keys_scales, lam, width, old, offs, offs2, offs3):
    idx = unstriped8(offs)
    idx2 = unstriped8(offs2)
    idx3 = unstriped8(offs3)
    keysu = unpack_weight(keys_words, keys_scales, "e2m1")
    queryq = mxq(f64(query), 0, "e4m3")
    a = queryq.T @ keysu
    query2q = mxq(f64(query2), 0, "e4m3")
    b = query2q.T @ keysu
    s = (np.maximum(pick8(a, idx, 16), pick8(b, idx2, 16)) - np.maximum(pick8(a, idx2, 16), pick8(b, idx, 16))) * f64(lam)
    ce = (s - np.mean(s, axis=1, keepdims=True)) / f64(width)
    p = 1.0 / (np.square(ce) + 1.0)
    w = p / np.sum(p, axis=1, keepdims=True)
    ws = w * 512.0
    f1 = np.zeros((Q, T))
    f1[np.arange(Q)[:, None], idx[np.arange(Q) % 128 // 16]] = ws
    f2 = f1 + f64(old)
    y = pick8(f2, idx3, 16)
    return y

@@ -1,0 +1,158 @@
+from contextlib import ExitStack
+
+import concourse.mybir as mybir
+
+D, T, I, Q = 512, 1024, 512, 128
+FLOPS = 2 * 2 * D * Q * T
+
+F32 = mybir.dt.float32
+BF16 = mybir.dt.bfloat16
+I32 = mybir.dt.int32
+U32 = mybir.dt.uint32
+U16 = mybir.dt.uint16
+U8 = mybir.dt.uint8
+FP8X4 = mybir.dt.float8_e4m3fn_x4
+FP4X4 = mybir.dt.float4_e2m1fn_x4
+ALU = mybir.AluOpType
+ACT = mybir.ActivationFunctionType
+
+P = 128
+PACK = 4
+N = 256
+H = I // 2
+LC = I // 16
+SPLIT = 320
+
+
+def tile_attend_exchanged_typical_through_heads_kernel(
+    tc, query, query2, keys_words, keys_scales, lam, width, old, offs, offs2, offs3, out
+):
+    nc = tc.nc
+    with ExitStack() as ctx:
+        sb = ctx.enter_context(tc.tile_pool(name="sb", bufs=1))
+        ps = ctx.enter_context(tc.psum_pool(name="ps", bufs=1))
+
+        list1 = sb.tile([P, LC], U16, name="list1")
+        list2 = sb.tile([P, LC], U16, name="list2")
+        list3 = sb.tile([P, LC], U16, name="list3")
+        q_raw = [sb.tile([P, PACK, Q], F32, name="q_raw%d" % j) for j in range(2)]
+        words = sb.tile([P, 2 * T], U8, name="words", align_bytes=64)
+        k_scales = sb.tile([P, T], U8, name="k_scales", align_bytes=64)
+        lam_sb = sb.tile([P, 1], F32, name="lam_sb")
+        width_sb = sb.tile([P, 1], F32, name="width_sb")
+        old_sb = sb.tile([P, T], F32, name="old_sb")
+        f1 = sb.tile([P, T], F32, name="f1")
+
+        nc.sync.dma_start(out=q_raw[0][:], in_=query.rearrange("(p j) q -> p j q", j=PACK))
+        for g in range(4):
+            nc.scalar.dma_start(
+                out=k_scales[32 * g : 32 * g + 4, :].bitcast(I32),
+                in_=keys_scales[0, 4 * g : 4 * g + 4, :].bitcast(I32),
+            )
+        nc.sync.dma_start(out=words[:], in_=keys_words[0])
+        nc.sync.dma_start(out=q_raw[1][:], in_=query2.rearrange("(p j) q -> p j q", j=PACK))
+        nc.gpsimd.dma_start(out=width_sb[:], in_=width)
+        nc.gpsimd.dma_start(out=lam_sb[:], in_=lam)
+        nc.sync.dma_start(out=list1[:], in_=offs)
+        nc.sync.dma_start(out=list2[:], in_=offs2)
+        nc.sync.dma_start(out=old_sb[:], in_=old)
+        nc.sync.dma_start(out=list3[:], in_=offs3)
+        nc.vector.memset(f1[:], 0.0)
+
+        inv_width = sb.tile([P, 1], F32, name="inv_width")
+        nc.scalar.activation(inv_width[:], width_sb[:], ACT.Abs_reciprocal_sqrt, scale=width_sb[:])
+        k1 = sb.tile([P, 1], F32, name="k1")
+        k2 = sb.tile([P, 1], F32, name="k2")
+        nc.gpsimd.tensor_scalar(k1[:], inv_width[:], lam_sb[:], 1.0 / I, ALU.mult, ALU.mult)
+        nc.gpsimd.tensor_tensor(k2[:], k1[:], k1[:], ALU.mult)
+
+        scores = []
+        banks = []
+        for j in range(2):
+            grouped = sb.tile([P, Q, PACK], BF16, name="grouped%d" % j, align_bytes=64)
+            src = q_raw[j][:].rearrange("p j q -> p q j")
+            if j == 0:
+                nc.vector.tensor_copy(grouped[:], src)
+            else:
+                nc.scalar.copy(grouped[:], src)
+            codes = sb.tile([P, Q], U32, name="codes%d" % j, align_bytes=64)
+            q_scales = sb.tile([P, Q], U8, name="q_scales%d" % j, align_bytes=64)
+            nc.vector.quantize_mx(
+                out=codes[:].bitcast(FP8X4),
+                scales=q_scales[:],
+                in_=grouped[:].rearrange("p q j -> p (q j)"),
+            )
+            row = []
+            for c in range(T // N):
+                bank = ps.tile([P, N], F32, name="bank%d_%d" % (j, c))
+                nc.tensor.matmul_mx(
+                    out=bank[:],
+                    lhsT=codes[:].bitcast(FP8X4),
+                    lhsT_scale=q_scales[:],
+                    rhs=words[:, 2 * N * c : 2 * N * (c + 1)].bitcast(FP4X4),
+                    rhs_scale=k_scales[:, N * c : N * (c + 1)],
+                    start=True,
+                    stop=True,
+                )
+                row.append(bank)
+            banks.append(row)
+            scores.append(sb.tile([P, T], F32, name="score%d" % j))
+        a, b = scores
+        for c in range(T // N):
+            cols = slice(N * c, N * (c + 1))
+            if c % 2 == 0:
+                nc.scalar.copy(a[:, cols], banks[0][c][:])
+            else:
+                nc.vector.tensor_copy(a[:, cols], banks[0][c][:])
+        for c in range(T // N):
+            nc.scalar.copy(b[:, N * c : N * (c + 1)], banks[1][c][:])
+
+        a1 = sb.tile([P, I], F32, name="a1")
+        a2 = sb.tile([P, I], F32, name="a2")
+        b1 = sb.tile([P, I], F32, name="b1")
+        b2 = sb.tile([P, I], F32, name="b2")
+        m1 = sb.tile([P, I], F32, name="m1")
+        m2 = sb.tile([P, I], F32, name="m2")
+        diff = sb.tile([P, I], F32, name="diff")
+        dsum = sb.tile([P, 1], F32, name="dsum")
+        halves = [(slice(H * h, H * (h + 1)), slice(LC // 2 * h, LC // 2 * (h + 1))) for h in range(2)]
+
+        (s0, e0), (s1, e1) = halves
+        nc.vector.tensor_copy(a1[:], a[:].indirect(list1[:]))
+        nc.scalar.activation(a2[:, s0], a[:].indirect(list2[:, e0]), ACT.Copy)
+        nc.vector.tensor_copy(b2[:], b[:].indirect(list2[:]))
+        nc.scalar.activation(b1[:, s0], b[:].indirect(list1[:, e0]), ACT.Copy)
+        nc.vector.tensor_tensor(m1[:], a1[:], b2[:], ALU.max)
+        nc.scalar.activation(a2[:, s1], a[:].indirect(list2[:, e1]), ACT.Copy)
+        nc.vector.tensor_copy(b1[:, s1], b[:].indirect(list1[:, e1]))
+        nc.vector.tensor_tensor(m2[:], a2[:], b1[:], ALU.max)
+        nc.vector.scalar_tensor_tensor(diff[:], m1[:], 1.0, m2[:], ALU.mult, ALU.subtract, accum_out=dsum[:])
+
+        sq = sb.tile([P, I], F32, name="sq")
+        cen = sb.tile([P, I - SPLIT], F32, name="cen")
+        u = sb.tile([P, I], F32, name="u")
+        part = sb.tile([P, I], F32, name="part")
+        sum0 = sb.tile([P, 1], F32, name="sum0")
+        sum1 = sb.tile([P, 1], F32, name="sum1")
+        root = sb.tile([P, 1], F32, name="root")
+        lo = slice(0, SPLIT)
+        hi = slice(SPLIT, I)
+        nc.scalar.activation(sq[:, lo], diff[:, lo], ACT.Square, bias=dsum[:], scale=-float(I))
+        nc.vector.tensor_scalar(cen[:], diff[:, hi], -float(I), dsum[:], ALU.mult, ALU.add)
+        nc.vector.tensor_tensor(sq[:, hi], cen[:], cen[:], ALU.mult)
+        nc.scalar.activation(u[:, lo], sq[:, lo], ACT.Abs_reciprocal_sqrt, bias=1.0, scale=k2[:])
+        nc.scalar.activation(u[:, hi], sq[:, hi], ACT.Abs_reciprocal_sqrt, bias=1.0, scale=k2[:])
+        nc.vector.scalar_tensor_tensor(part[:, lo], u[:, lo], 1.0 / I, u[:, lo], ALU.mult, ALU.mult, accum_out=sum0[:])
+        nc.scalar.activation(part[:, hi], u[:, hi], ACT.Square, accum_out=sum1[:])
+        nc.scalar.activation(root[:], sum1[:], ACT.Abs_reciprocal_sqrt, bias=sum0[:], scale=1.0 / I)
+        v = sb.tile([P, I], F32, name="v")
+        nc.vector.tensor_scalar(v[:], u[:], root[:], None, ALU.mult)
+        nc.vector.tensor_tensor(f1[:].indirect(list1[:]), v[:], v[:], ALU.mult)
+
+        f2 = sb.tile([P, T], F32, name="f2")
+        nc.vector.tensor_tensor(f2[:], f1[:], old_sb[:], ALU.add)
+        y = [sb.tile([P, H], F32, name="y%d" % h) for h in range(2)]
+        nc.vector.tensor_copy(y[0][:], f2[:].indirect(list3[:, halves[0][1]]))
+        nc.scalar.activation(y[1][:], f2[:].indirect(list3[:, halves[1][1]]), ACT.Copy)
+        nc.sync.dma_start(out=out[:, halves[0][0]], in_=y[0][:])
+        nc.scalar.dma_start(out=out[:, halves[1][0]], in_=y[1][:])

@@ -21,7 +21,7 @@ PACK = 4
 N = 256
 H = I // 2
 LC = I // 16
-SPLIT = 320
+PA, PC = 160, 160
 
 
 def tile_attend_exchanged_typical_through_heads_kernel(
@@ -36,7 +36,7 @@ def tile_attend_exchanged_typical_through_heads_kernel(
         list2 = sb.tile([P, LC], U16, name="list2")
         list3 = sb.tile([P, LC], U16, name="list3")
         q_raw = [sb.tile([P, PACK, Q], F32, name="q_raw%d" % j) for j in range(2)]
-        words = sb.tile([P, 2 * T], U8, name="words", align_bytes=64)
+        words = [sb.tile([P, T], U8, name="words%d" % h, align_bytes=64) for h in range(2)]
         k_scales = sb.tile([P, T], U8, name="k_scales", align_bytes=64)
         lam_sb = sb.tile([P, 1], F32, name="lam_sb")
         width_sb = sb.tile([P, 1], F32, name="width_sb")
@@ -45,16 +45,17 @@ def tile_attend_exchanged_typical_through_heads_kernel(
 
         nc.sync.dma_start(out=q_raw[0][:], in_=query.rearrange("(p j) q -> p j q", j=PACK))
         for g in range(4):
-            nc.scalar.dma_start(
+            (nc.sync if g < 2 else nc.scalar).dma_start(
                 out=k_scales[32 * g : 32 * g + 4, :].bitcast(I32),
                 in_=keys_scales[0, 4 * g : 4 * g + 4, :].bitcast(I32),
             )
-        nc.sync.dma_start(out=words[:], in_=keys_words[0])
+        nc.sync.dma_start(out=words[0][:], in_=keys_words[0, :, :T])
         nc.sync.dma_start(out=q_raw[1][:], in_=query2.rearrange("(p j) q -> p j q", j=PACK))
+        nc.sync.dma_start(out=words[1][:], in_=keys_words[0, :, T:])
         nc.gpsimd.dma_start(out=width_sb[:], in_=width)
-        nc.gpsimd.dma_start(out=lam_sb[:], in_=lam)
         nc.sync.dma_start(out=list1[:], in_=offs)
         nc.sync.dma_start(out=list2[:], in_=offs2)
+        nc.sync.dma_start(out=lam_sb[:], in_=lam)
         nc.sync.dma_start(out=old_sb[:], in_=old)
         nc.sync.dma_start(out=list3[:], in_=offs3)
         nc.vector.memset(f1[:], 0.0)
@@ -70,18 +71,17 @@ def tile_attend_exchanged_typical_through_heads_kernel(
         banks = []
         for j in range(2):
             grouped = sb.tile([P, Q, PACK], BF16, name="grouped%d" % j, align_bytes=64)
-            src = q_raw[j][:].rearrange("p j q -> p q j")
-            if j == 0:
-                nc.vector.tensor_copy(grouped[:], src)
-            else:
-                nc.scalar.copy(grouped[:], src)
             codes = sb.tile([P, Q], U32, name="codes%d" % j, align_bytes=64)
             q_scales = sb.tile([P, Q], U8, name="q_scales%d" % j, align_bytes=64)
-            nc.vector.quantize_mx(
-                out=codes[:].bitcast(FP8X4),
-                scales=q_scales[:],
-                in_=grouped[:].rearrange("p q j -> p (q j)"),
-            )
+            rows = [slice(0, Q // 2), slice(Q // 2, Q)]
+            for r in rows:
+                nc.vector.tensor_copy(grouped[:, r, :], q_raw[j][:, :, r].rearrange("p j q -> p q j"))
+            for r in rows:
+                nc.vector.quantize_mx(
+                    out=codes[:, r].bitcast(FP8X4),
+                    scales=q_scales[:, r],
+                    in_=grouped[:, r, :].rearrange("p q j -> p (q j)"),
+                )
             row = []
             for c in range(T // N):
                 bank = ps.tile([P, N], F32, name="bank%d_%d" % (j, c))
@@ -89,7 +89,7 @@ def tile_attend_exchanged_typical_through_heads_kernel(
                     out=bank[:],
                     lhsT=codes[:].bitcast(FP8X4),
                     lhsT_scale=q_scales[:],
-                    rhs=words[:, 2 * N * c : 2 * N * (c + 1)].bitcast(FP4X4),
+                    rhs=words[c // 2][:, 2 * N * (c % 2) : 2 * N * (c % 2 + 1)].bitcast(FP4X4),
                     rhs_scale=k_scales[:, N * c : N * (c + 1)],
                     start=True,
                     stop=True,
@@ -100,13 +100,7 @@ def tile_attend_exchanged_typical_through_heads_kernel(
         a, b = scores
         for c in range(T // N):
             cols = slice(N * c, N * (c + 1))
-            if c % 2 == 0:
-                nc.scalar.copy(a[:, cols], banks[0][c][:])
-            else:
-                nc.vector.tensor_copy(a[:, cols], banks[0][c][:])
-        for c in range(T // N):
-            nc.scalar.copy(b[:, N * c : N * (c + 1)], banks[1][c][:])
-
+            nc.scalar.copy(a[:, cols], banks[0][c][:])
         a1 = sb.tile([P, I], F32, name="a1")
         a2 = sb.tile([P, I], F32, name="a2")
         b1 = sb.tile([P, I], F32, name="b1")
@@ -118,32 +112,39 @@ def tile_attend_exchanged_typical_through_heads_kernel(
         halves = [(slice(H * h, H * (h + 1)), slice(LC // 2 * h, LC // 2 * (h + 1))) for h in range(2)]
 
         (s0, e0), (s1, e1) = halves
-        nc.vector.tensor_copy(a1[:], a[:].indirect(list1[:]))
-        nc.scalar.activation(a2[:, s0], a[:].indirect(list2[:, e0]), ACT.Copy)
-        nc.vector.tensor_copy(b2[:], b[:].indirect(list2[:]))
-        nc.scalar.activation(b1[:, s0], b[:].indirect(list1[:, e0]), ACT.Copy)
-        nc.vector.tensor_tensor(m1[:], a1[:], b2[:], ALU.max)
+        nc.scalar.activation(a1[:, s0], a[:].indirect(list1[:, e0]), ACT.Copy)
+        for c in range(T // N):
+            nc.vector.tensor_copy(b[:, N * c : N * (c + 1)], banks[1][c][:])
+        nc.scalar.activation(a1[:, s1], a[:].indirect(list1[:, e1]), ACT.Copy)
         nc.scalar.activation(a2[:, s1], a[:].indirect(list2[:, e1]), ACT.Copy)
-        nc.vector.tensor_copy(b1[:, s1], b[:].indirect(list1[:, e1]))
-        nc.vector.tensor_tensor(m2[:], a2[:], b1[:], ALU.max)
+        nc.vector.tensor_tensor(a2[:, s0], a[:].indirect(list2[:, e0]), a1[:, s0], ALU.subtract)
+        nc.vector.tensor_tensor(b2[:, s0], b[:].indirect(list2[:, e0]), a1[:, s0], ALU.subtract)
+        nc.vector.tensor_tensor(b1[:, s0], b[:].indirect(list1[:, e0]), a1[:, s0], ALU.subtract)
+        nc.scalar.activation(b2[:, s1], b[:].indirect(list2[:, e1]), ACT.Copy)
+        nc.scalar.activation(b1[:, s1], b[:].indirect(list1[:, e1]), ACT.Copy)
+        nc.scalar.activation(m1[:, s0], b2[:, s0], ACT.Relu)
+        nc.vector.tensor_tensor(m1[:, s1], a1[:, s1], b2[:, s1], ALU.max)
+        nc.vector.tensor_tensor(m2[:, s0], a2[:, s0], b1[:, s0], ALU.max)
+        nc.vector.tensor_tensor(m2[:, s1], a2[:, s1], b1[:, s1], ALU.max)
         nc.vector.scalar_tensor_tensor(diff[:], m1[:], 1.0, m2[:], ALU.mult, ALU.subtract, accum_out=dsum[:])
 
         sq = sb.tile([P, I], F32, name="sq")
-        cen = sb.tile([P, I - SPLIT], F32, name="cen")
+        cen = sb.tile([P, PC], F32, name="cen")
         u = sb.tile([P, I], F32, name="u")
         part = sb.tile([P, I], F32, name="part")
         sum0 = sb.tile([P, 1], F32, name="sum0")
         sum1 = sb.tile([P, 1], F32, name="sum1")
         root = sb.tile([P, 1], F32, name="root")
-        lo = slice(0, SPLIT)
-        hi = slice(SPLIT, I)
-        nc.scalar.activation(sq[:, lo], diff[:, lo], ACT.Square, bias=dsum[:], scale=-float(I))
-        nc.vector.tensor_scalar(cen[:], diff[:, hi], -float(I), dsum[:], ALU.mult, ALU.add)
-        nc.vector.tensor_tensor(sq[:, hi], cen[:], cen[:], ALU.mult)
-        nc.scalar.activation(u[:, lo], sq[:, lo], ACT.Abs_reciprocal_sqrt, bias=1.0, scale=k2[:])
-        nc.scalar.activation(u[:, hi], sq[:, hi], ACT.Abs_reciprocal_sqrt, bias=1.0, scale=k2[:])
-        nc.vector.scalar_tensor_tensor(part[:, lo], u[:, lo], 1.0 / I, u[:, lo], ALU.mult, ALU.mult, accum_out=sum0[:])
-        nc.scalar.activation(part[:, hi], u[:, hi], ACT.Square, accum_out=sum1[:])
+        pa, pc, pb = slice(0, PA), slice(PA, PA + PC), slice(PA + PC, I)
+        pac = slice(0, PA + PC)
+        nc.scalar.activation(sq[:, pa], diff[:, pa], ACT.Square, bias=dsum[:], scale=-float(I))
+        nc.vector.tensor_scalar(cen[:], diff[:, pc], -float(I), dsum[:], ALU.mult, ALU.add)
+        nc.scalar.activation(sq[:, pb], diff[:, pb], ACT.Square, bias=dsum[:], scale=-float(I))
+        nc.vector.tensor_tensor(sq[:, pc], cen[:], cen[:], ALU.mult)
+        for piece in (pa, pc, pb):
+            nc.scalar.activation(u[:, piece], sq[:, piece], ACT.Abs_reciprocal_sqrt, bias=1.0, scale=k2[:])
+        nc.vector.scalar_tensor_tensor(part[:, pb], u[:, pb], 1.0 / I, u[:, pb], ALU.mult, ALU.mult, accum_out=sum0[:])
+        nc.scalar.activation(part[:, pac], u[:, pac], ACT.Square, accum_out=sum1[:])
         nc.scalar.activation(root[:], sum1[:], ACT.Abs_reciprocal_sqrt, bias=sum0[:], scale=1.0 / I)
         v = sb.tile([P, I], F32, name="v")
         nc.vector.tensor_scalar(v[:], u[:], root[:], None, ALU.mult)

from contextlib import ExitStack

import concourse.mybir as mybir

D, T, I, Q = 512, 1024, 512, 128
FLOPS = 2 * 2 * D * Q * T

F32 = mybir.dt.float32
BF16 = mybir.dt.bfloat16
I32 = mybir.dt.int32
U32 = mybir.dt.uint32
U16 = mybir.dt.uint16
U8 = mybir.dt.uint8
FP8X4 = mybir.dt.float8_e4m3fn_x4
FP4X4 = mybir.dt.float4_e2m1fn_x4
ALU = mybir.AluOpType
ACT = mybir.ActivationFunctionType

P = 128
PACK = 4
N = 256
H = I // 2
LC = I // 16
PA, PC = 160, 160


def tile_attend_exchanged_typical_through_heads_kernel(
    tc, query, query2, keys_words, keys_scales, lam, width, old, offs, offs2, offs3, out
):
    nc = tc.nc
    with ExitStack() as ctx:
        sb = ctx.enter_context(tc.tile_pool(name="sb", bufs=1))
        ps = ctx.enter_context(tc.psum_pool(name="ps", bufs=1))

        list1 = sb.tile([P, LC], U16, name="list1")
        list2 = sb.tile([P, LC], U16, name="list2")
        list3 = sb.tile([P, LC], U16, name="list3")
        q_raw = [sb.tile([P, PACK, Q], F32, name="q_raw%d" % j) for j in range(2)]
        words = [sb.tile([P, T], U8, name="words%d" % h, align_bytes=64) for h in range(2)]
        k_scales = sb.tile([P, T], U8, name="k_scales", align_bytes=64)
        lam_sb = sb.tile([P, 1], F32, name="lam_sb")
        width_sb = sb.tile([P, 1], F32, name="width_sb")
        old_sb = sb.tile([P, T], F32, name="old_sb")
        f1 = sb.tile([P, T], F32, name="f1")

        nc.sync.dma_start(out=q_raw[0][:], in_=query.rearrange("(p j) q -> p j q", j=PACK))
        for g in range(4):
            (nc.sync if g < 2 else nc.scalar).dma_start(
                out=k_scales[32 * g : 32 * g + 4, :].bitcast(I32),
                in_=keys_scales[0, 4 * g : 4 * g + 4, :].bitcast(I32),
            )
        nc.sync.dma_start(out=words[0][:], in_=keys_words[0, :, :T])
        nc.sync.dma_start(out=q_raw[1][:], in_=query2.rearrange("(p j) q -> p j q", j=PACK))
        nc.sync.dma_start(out=words[1][:], in_=keys_words[0, :, T:])
        nc.gpsimd.dma_start(out=width_sb[:], in_=width)
        nc.sync.dma_start(out=list1[:], in_=offs)
        nc.sync.dma_start(out=list2[:], in_=offs2)
        nc.sync.dma_start(out=lam_sb[:], in_=lam)
        nc.sync.dma_start(out=old_sb[:], in_=old)
        nc.sync.dma_start(out=list3[:], in_=offs3)
        nc.vector.memset(f1[:], 0.0)

        inv_width = sb.tile([P, 1], F32, name="inv_width")
        nc.scalar.activation(inv_width[:], width_sb[:], ACT.Abs_reciprocal_sqrt, scale=width_sb[:])
        k1 = sb.tile([P, 1], F32, name="k1")
        k2 = sb.tile([P, 1], F32, name="k2")
        nc.gpsimd.tensor_scalar(k1[:], inv_width[:], lam_sb[:], 1.0 / I, ALU.mult, ALU.mult)
        nc.gpsimd.tensor_tensor(k2[:], k1[:], k1[:], ALU.mult)

        scores = []
        banks = []
        for j in range(2):
            grouped = sb.tile([P, Q, PACK], BF16, name="grouped%d" % j, align_bytes=64)
            codes = sb.tile([P, Q], U32, name="codes%d" % j, align_bytes=64)
            q_scales = sb.tile([P, Q], U8, name="q_scales%d" % j, align_bytes=64)
            rows = [slice(0, Q // 2), slice(Q // 2, Q)]
            for r in rows:
                nc.vector.tensor_copy(grouped[:, r, :], q_raw[j][:, :, r].rearrange("p j q -> p q j"))
            for r in rows:
                nc.vector.quantize_mx(
                    out=codes[:, r].bitcast(FP8X4),
                    scales=q_scales[:, r],
                    in_=grouped[:, r, :].rearrange("p q j -> p (q j)"),
                )
            row = []
            for c in range(T // N):
                bank = ps.tile([P, N], F32, name="bank%d_%d" % (j, c))
                nc.tensor.matmul_mx(
                    out=bank[:],
                    lhsT=codes[:].bitcast(FP8X4),
                    lhsT_scale=q_scales[:],
                    rhs=words[c // 2][:, 2 * N * (c % 2) : 2 * N * (c % 2 + 1)].bitcast(FP4X4),
                    rhs_scale=k_scales[:, N * c : N * (c + 1)],
                    start=True,
                    stop=True,
                )
                row.append(bank)
            banks.append(row)
            scores.append(sb.tile([P, T], F32, name="score%d" % j))
        a, b = scores
        for c in range(T // N):
            cols = slice(N * c, N * (c + 1))
            nc.scalar.copy(a[:, cols], banks[0][c][:])
        a1 = sb.tile([P, I], F32, name="a1")
        a2 = sb.tile([P, I], F32, name="a2")
        b1 = sb.tile([P, I], F32, name="b1")
        b2 = sb.tile([P, I], F32, name="b2")
        m1 = sb.tile([P, I], F32, name="m1")
        m2 = sb.tile([P, I], F32, name="m2")
        diff = sb.tile([P, I], F32, name="diff")
        dsum = sb.tile([P, 1], F32, name="dsum")
        halves = [(slice(H * h, H * (h + 1)), slice(LC // 2 * h, LC // 2 * (h + 1))) for h in range(2)]

        (s0, e0), (s1, e1) = halves
        nc.scalar.activation(a1[:, s0], a[:].indirect(list1[:, e0]), ACT.Copy)
        for c in range(T // N):
            nc.vector.tensor_copy(b[:, N * c : N * (c + 1)], banks[1][c][:])
        nc.scalar.activation(a1[:, s1], a[:].indirect(list1[:, e1]), ACT.Copy)
        nc.scalar.activation(a2[:, s1], a[:].indirect(list2[:, e1]), ACT.Copy)
        nc.vector.tensor_tensor(a2[:, s0], a[:].indirect(list2[:, e0]), a1[:, s0], ALU.subtract)
        nc.vector.tensor_tensor(b2[:, s0], b[:].indirect(list2[:, e0]), a1[:, s0], ALU.subtract)
        nc.vector.tensor_tensor(b1[:, s0], b[:].indirect(list1[:, e0]), a1[:, s0], ALU.subtract)
        nc.scalar.activation(b2[:, s1], b[:].indirect(list2[:, e1]), ACT.Copy)
        nc.scalar.activation(b1[:, s1], b[:].indirect(list1[:, e1]), ACT.Copy)
        nc.scalar.activation(m1[:, s0], b2[:, s0], ACT.Relu)
        nc.vector.tensor_tensor(m1[:, s1], a1[:, s1], b2[:, s1], ALU.max)
        nc.vector.tensor_tensor(m2[:, s0], a2[:, s0], b1[:, s0], ALU.max)
        nc.vector.tensor_tensor(m2[:, s1], a2[:, s1], b1[:, s1], ALU.max)
        nc.vector.scalar_tensor_tensor(diff[:], m1[:], 1.0, m2[:], ALU.mult, ALU.subtract, accum_out=dsum[:])

        sq = sb.tile([P, I], F32, name="sq")
        cen = sb.tile([P, PC], F32, name="cen")
        u = sb.tile([P, I], F32, name="u")
        part = sb.tile([P, I], F32, name="part")
        sum0 = sb.tile([P, 1], F32, name="sum0")
        sum1 = sb.tile([P, 1], F32, name="sum1")
        root = sb.tile([P, 1], F32, name="root")
        pa, pc, pb = slice(0, PA), slice(PA, PA + PC), slice(PA + PC, I)
        pac = slice(0, PA + PC)
        nc.scalar.activation(sq[:, pa], diff[:, pa], ACT.Square, bias=dsum[:], scale=-float(I))
        nc.vector.tensor_scalar(cen[:], diff[:, pc], -float(I), dsum[:], ALU.mult, ALU.add)
        nc.scalar.activation(sq[:, pb], diff[:, pb], ACT.Square, bias=dsum[:], scale=-float(I))
        nc.vector.tensor_tensor(sq[:, pc], cen[:], cen[:], ALU.mult)
        for piece in (pa, pc, pb):
            nc.scalar.activation(u[:, piece], sq[:, piece], ACT.Abs_reciprocal_sqrt, bias=1.0, scale=k2[:])
        nc.vector.scalar_tensor_tensor(part[:, pb], u[:, pb], 1.0 / I, u[:, pb], ALU.mult, ALU.mult, accum_out=sum0[:])
        nc.scalar.activation(part[:, pac], u[:, pac], ACT.Square, accum_out=sum1[:])
        nc.scalar.activation(root[:], sum1[:], ACT.Abs_reciprocal_sqrt, bias=sum0[:], scale=1.0 / I)
        v = sb.tile([P, I], F32, name="v")
        nc.vector.tensor_scalar(v[:], u[:], root[:], None, ALU.mult)
        nc.vector.tensor_tensor(f1[:].indirect(list1[:]), v[:], v[:], ALU.mult)

        f2 = sb.tile([P, T], F32, name="f2")
        nc.vector.tensor_tensor(f2[:], f1[:], old_sb[:], ALU.add)
        y = [sb.tile([P, H], F32, name="y%d" % h) for h in range(2)]
        nc.vector.tensor_copy(y[0][:], f2[:].indirect(list3[:, halves[0][1]]))
        nc.scalar.activation(y[1][:], f2[:].indirect(list3[:, halves[1][1]]), ACT.Copy)
        nc.sync.dma_start(out=out[:, halves[0][0]], in_=y[0][:])
        nc.scalar.dma_start(out=out[:, halves[1][0]], in_=y[1][:])
